import numpy as np
import ml_dtypes


def mxq(x, axis, fmt="e4m3"):
    dtype, down = {"e4m3": (ml_dtypes.float8_e4m3fn, 7), "e5m2": (ml_dtypes.float8_e5m2, 14)}[fmt]
    v = np.moveaxis(np.asarray(x, np.float32).astype(ml_dtypes.bfloat16).astype(np.float64), axis, -1)
    blocks = v.reshape(v.shape[:-1] + (-1, 32))
    amax = np.abs(blocks).max(-1, keepdims=True)
    byte = np.maximum(np.where(amax > 0, np.frexp(amax)[1] - 1 + 127, 0) - down, 1)
    scale = np.exp2(byte - 127.0)
    codes = (blocks / scale).astype(np.float32).astype(dtype).astype(np.float64)
    return np.moveaxis((codes * scale).reshape(v.shape), -1, axis)


WIDE = False


def mx_kscale(k):
    if not WIDE:
        return np.ones(k)
    levels = np.array([10, -10, 5, -5, 0])
    if k % 512:
        return np.exp2(np.random.permutation(np.resize(levels, k // 32))).repeat(32)
    a = np.empty((k // 512, 16))
    for p in range(k // 512):
        a[p, :8] = np.random.permutation(np.resize(levels, 8))
        for g in range(8):
            far = levels[np.abs(levels - a[p, g]) >= 10]
            a[p, g + 8] = far[np.random.randint(len(far))]
    return np.exp2(a.ravel()).repeat(32)


def f64(x):
    return np.asarray(x).astype(np.float64)


def striped(idx):
    return np.tile(idx.reshape(-1, 16).T, (8, 1)).astype(np.uint16)


def unstriped(offs):
    return offs[:16].T.reshape(-1).astype(np.int64)


def striped8(idx):
    return np.concatenate([x.reshape(-1, 16).T for x in idx]).astype(np.uint16)


def runs(offs, k):
    lists = np.stack([offs[16 * r : 16 * r + 16].T.reshape(-1) for r in range(8)]).astype(np.int64)
    return lists[np.arange(k) % 512 // 64]


def pack_weight(w):
    k, n = w.shape
    w = f64(np.asarray(w, np.float32).astype(ml_dtypes.bfloat16)).reshape(k // 32, 32, n)
    amax = np.abs(w).max(1)
    byte = np.clip(np.where(amax > 0, np.frexp(amax)[1] - 1 + 127 - 7, 1), 1, 254)
    scaled = (w * np.exp2(127.0 - byte)[:, None, :]).reshape(k, n).astype(np.float32)
    words = np.ascontiguousarray(scaled.reshape(k // 512, 128, 4, n).transpose(0, 1, 3, 2)).astype(ml_dtypes.float8_e4m3fn).view(np.uint8)
    return words, np.ascontiguousarray(byte.astype(np.uint8).reshape(k // 512, 16, n))


def unpack_weight(words, scales):
    g, p, n, _ = words.shape
    vals = np.ascontiguousarray(words).view(ml_dtypes.float8_e4m3fn).astype(np.float64) * np.repeat(np.exp2(scales.astype(np.float64) - 127.0), 8, axis=1)[..., None]
    return vals.transpose(0, 1, 3, 2).reshape(g * 512, n)


K, T, S, N, G, H, W = 512, 2048, 512, 512, 2048, 512, 256


def setup_inputs():
    n = np.random.standard_normal
    s = mx_kscale(K)[:, None]
    u = mx_kscale(S)
    packed_xT = pack_weight(n((K, T)) * s)
    packed_dT = pack_weight(n((K, G)) / s)
    perm = np.stack([np.random.permutation(S) for _ in range(8)])
    return {
        "x_words": packed_xT[0],
        "x_scales": packed_xT[1],
        "d_words": packed_dT[0],
        "d_scales": packed_dT[1],
        "gn": (np.random.uniform(0.5, 1.5, (H, 1)) * u[:, None]).astype(np.float32),
        "w1": (n((H, N)) / np.sqrt(H) / u[:, None]).astype(np.float32),
        "offs": striped8(np.random.randint(0, T, (8, S))),
        "ci": striped(np.random.permutation(G)[:H]),
        "n1": striped8(perm[:, :W]),
        "n2": striped8(perm[:, W:]),
        "n3": striped8(np.stack([np.random.permutation(S) for _ in range(8)])),
        "n4": striped8(np.stack([np.random.permutation(S) for _ in range(8)])),
    }


def reference(x_words, x_scales, d_words, d_scales, gn, w1, offs, ci, n1, n2, n3, n4):
    d_ci = unpack_weight(d_words, d_scales)[:, unstriped(ci)]
    xq = unpack_weight(x_words, x_scales)[np.arange(K)[:, None], runs(offs, K)]
    s = 0.0625 * (d_ci.T @ xq)
    pa = s[np.arange(H)[:, None], runs(n1, H)]
    pb = s[np.arange(H)[:, None], runs(n2, H)]
    rb = np.maximum(pa, pb)
    ra = pa / (np.abs(pb) + 0.5)
    ds = np.zeros((H, S))
    ds[np.arange(H)[:, None], runs(n1, H)] = ra
    dt = ds.copy()
    dt[np.arange(H)[:, None], runs(n2, H)] = rb
    z = f64(gn) * dt
    h = mxq(f64(w1), 0, "e4m3").T @ mxq(z, 0, "e4m3")
    st = np.maximum(h, h[np.arange(N)[:, None], runs(n3, N)])
    ds2 = np.zeros((N, S))
    ds2[np.arange(N)[:, None], runs(n4, N)] = st
    return ds2 - h

@@ -1,0 +1,186 @@
+from contextlib import ExitStack
+
+import concourse.mybir as mybir
+
+F32 = mybir.dt.float32
+BF16 = mybir.dt.bfloat16
+I32 = mybir.dt.int32
+U32 = mybir.dt.uint32
+U16 = mybir.dt.uint16
+U8 = mybir.dt.uint8
+FP8X4 = mybir.dt.float8_e4m3fn_x4
+ALU = mybir.AluOpType
+ACT = mybir.ActivationFunctionType
+
+P = 128
+PACK = 4
+TABLE = 2048
+S = 512
+HALF = 256
+FLOPS = 2 * 2 * 512 * 512 * 512
+
+
+def tile_picked_hwlratiosendhop_none_p_kernel(tc, x_words, x_scales, d_words, d_scales, gn, w1, offs, ci, n1, n2, n3, n4, out):
+    nc = tc.nc
+    with ExitStack() as ctx:
+        keep = ctx.enter_context(tc.tile_pool(name="keep", bufs=1))
+        psum = ctx.enter_context(tc.psum_pool(name="psum", bufs=1))
+
+        def load_list(name, src):
+            tile = keep.tile(list(src.shape), U16, name=name)
+            nc.sync.dma_start(tile[:], src)
+            return tile
+
+        def cols(half):
+            return slice(half * HALF, (half + 1) * HALF)
+
+        def entries(half):
+            return slice(half * HALF // 16, (half + 1) * HALF // 16)
+
+        def rows(t):
+            return slice(t * P, (t + 1) * P)
+
+        xs_tab = keep.tile([P, TABLE], U8, name="xs_tab")
+        ds_tab = keep.tile([P, TABLE], U8, name="ds_tab")
+        nc.gpsimd.memset(xs_tab[:].bitcast(I32), 0)
+        nc.vector.memset(ds_tab[:].bitcast(I32), 0)
+
+        offs_t = load_list("offs_t", offs)
+        ci_t = load_list("ci_t", ci)
+        n2_t = load_list("n2_t", n2)
+        n1_t = load_list("n1_t", n1)
+        nc.gpsimd.dma_start(xs_tab[:].bitcast(I32)[0:P:8, :], x_scales[0].bitcast(I32))
+        dw_tab = keep.tile([P, TABLE], U32, name="dw_tab", tag="dict_then_w1")
+        xw_tab = keep.tile([P, TABLE], U32, name="xw_tab")
+        nc.sync.dma_start(dw_tab[:].bitcast(I32), d_words[0].rearrange("p c r -> p (c r)").bitcast(I32))
+        n3_t = load_list("n3_t", n3)
+        n4_t = load_list("n4_t", n4)
+        for j in range(4):
+            nc.scalar.dma_start(ds_tab[:].bitcast(I32)[j:P:32, :], d_scales[0].bitcast(I32)[j:16:4, :])
+        nc.sync.dma_start(xw_tab[:].bitcast(I32), x_words[0].rearrange("p c r -> p (c r)").bitcast(I32))
+        gain = keep.tile([P, PACK], F32, name="gain")
+        nc.gpsimd.dma_start(gain[:], gn.rearrange("(p t) o -> p (t o)", t=PACK))
+
+        xs_pick = keep.tile([P, S], U8, name="xs_pick")
+        xs_plane = keep.tile([P, S], U8, name="xs_plane", align_bytes=64)
+        nc.vector.tensor_copy(xs_pick[:], xs_tab[:].indirect(offs_t[:]))
+        nc.vector.tensor_copy(xs_plane[:].bitcast(I32), xs_pick[:].bitcast(I32))
+        for j in range(1, 4):
+            nc.scalar.dma_start(xs_plane[:].bitcast(I32)[j:P:32, :], xs_pick[:].bitcast(I32)[8 * j : P : 32, :])
+        ds_pick = keep.tile([P, S], U8, name="ds_pick", align_bytes=64)
+        nc.vector.tensor_copy(ds_pick[:].rearrange("p (t m) -> p m t", t=PACK), ds_tab[:].indirect(ci_t[:]))
+        dw_pick = keep.tile([P, S], U32, name="dw_pick", align_bytes=64)
+        nc.vector.tensor_copy(dw_pick[:].rearrange("p (t m) -> p m t", t=PACK), dw_tab[:].indirect(ci_t[:]))
+        w_raw = keep.tile([P, PACK, S], F32, name="w_raw", tag="dict_then_w1")
+        nc.sync.dma_start(w_raw[:], w1.rearrange("(p j) n -> p j n", j=PACK))
+        xw_pick = keep.tile([P, S], U32, name="xw_pick", align_bytes=64)
+        for half in range(2):
+            nc.vector.tensor_copy(xw_pick[:, cols(half)], xw_tab[:].indirect(offs_t[:, entries(half)]))
+
+        def product(bank_names, lhs_words, lhs_scales, rhs_words, rhs_scales):
+            banks = []
+            for half in range(2):
+                bank = psum.tile([P, HALF], F32, name=bank_names[half])
+                nc.tensor.matmul_mx(out=bank[:], lhsT=lhs_words[:, rows(0)].bitcast(FP8X4), lhsT_scale=lhs_scales[:, rows(0)],
+                                    rhs=rhs_words[:, cols(half)].bitcast(FP8X4), rhs_scale=rhs_scales[:, cols(half)], start=True, stop=True)
+                banks.append(bank)
+            for t in range(1, PACK):
+                bank = psum.tile([P, S], F32, name=bank_names[t + 1])
+                nc.tensor.matmul_mx(out=bank[:], lhsT=lhs_words[:, rows(t)].bitcast(FP8X4), lhsT_scale=lhs_scales[:, rows(t)],
+                                    rhs=rhs_words[:].bitcast(FP8X4), rhs_scale=rhs_scales[:], start=True, stop=True)
+                banks.append(bank)
+            return banks
+
+        s_banks = product(["b0", "b1", "b2", "b3", "b4"], dw_pick, ds_pick, xw_pick, xs_plane)
+
+        def halves(name):
+            return [keep.tile([P, HALF], F32, name="%s%d" % (name, t)) for t in range(PACK)]
+
+        s_sb = [keep.tile([P, S], F32, name="s_sb%d" % t) for t in range(PACK)]
+        pa, pb, size, root, recip = halves("pa"), halves("pb"), halves("size"), halves("root"), halves("recip")
+        nc.scalar.activation(s_sb[0][:, cols(0)], s_banks[0][:], ACT.Copy, scale=0.0625)
+        nc.vector.tensor_scalar_mul(s_sb[0][:, cols(1)], s_banks[1][:], 0.0625)
+        nc.vector.tensor_copy(pa[0][:], s_sb[0][:].indirect(n1_t[:]))
+        nc.scalar.activation(pb[0][:], s_sb[0][:].indirect(n2_t[:]), ACT.Copy)
+        for t in range(PACK):
+            ahead = t + 1 < PACK
+            if ahead:
+                nc.scalar.activation(s_sb[t + 1][:], s_banks[t + 2][:], ACT.Copy, scale=0.0625)
+            nc.scalar.activation(size[t][:], pb[t][:], ACT.Abs)
+            if ahead:
+                nc.scalar.activation(pb[t + 1][:], s_sb[t + 1][:].indirect(n2_t[:]), ACT.Copy)
+            nc.scalar.activation(root[t][:], size[t][:], ACT.Abs_reciprocal_sqrt, bias=0.5)
+            if ahead:
+                nc.scalar.activation(pa[t + 1][:], s_sb[t + 1][:].indirect(n1_t[:]), ACT.Copy)
+            nc.scalar.activation(recip[t][:], root[t][:], ACT.Square)
+
+        z_planes = keep.tile([P, PACK, S], BF16, name="z_planes")
+        larger = halves("larger")
+        placed = [keep.tile([P, S], F32, name="placed%d" % t, align_bytes=64) for t in range(PACK)]
+        w_src = w_raw[:].rearrange("p j (m t) -> p m j t", t=PACK)
+
+        def weave_w1(w_il, quarters):
+            w_dst = w_il[:].rearrange("p (t m j) -> p m j t", t=PACK, j=PACK)
+            for q in quarters:
+                nc.scalar.copy(w_dst[:, 32 * q : 32 * q + 32], w_src[:, 32 * q : 32 * q + 32])
+
+        nc.vector.tensor_tensor(larger[0][:], pa[0][:], pb[0][:], ALU.max)
+        for t in range(PACK):
+            nc.vector.tensor_copy(placed[t][:].indirect(n2_t[:]), larger[t][:])
+            if t + 1 < PACK:
+                nc.vector.tensor_tensor(larger[t + 1][:], pa[t + 1][:], pb[t + 1][:], ALU.max)
+            nc.vector.tensor_tensor(placed[t][:].indirect(n1_t[:]), pa[t][:], recip[t][:], ALU.mult)
+            if t == 2:
+                w_il = keep.tile([P, PACK * S], BF16, name="w_il", tag="placed1", align_bytes=64)
+                weave_w1(w_il, (0, 1))
+            if t + 1 < PACK:
+                nc.scalar.activation(z_planes[:, t, :], placed[t][:], ACT.Copy, scale=gain[:, t : t + 1])
+            else:
+                nc.vector.tensor_scalar_mul(z_planes[:, t, :], placed[t][:], gain[:, t : t + 1])
+        weave_w1(w_il, (2, 3))
+
+        z_il = keep.tile([P, S * PACK], BF16, name="z_il", align_bytes=64)
+        z_words = keep.tile([P, S], U32, name="z_words", align_bytes=64)
+        z_scales = keep.tile([P, S], U8, name="z_scales", align_bytes=64)
+        w_words = keep.tile([P, S], U32, name="w_words", align_bytes=64)
+        w_scales = keep.tile([P, S], U8, name="w_scales", align_bytes=64)
+        z_dst = z_il[:].rearrange("p (c i t) -> p c t i", i=4, t=PACK)
+        z_src = z_planes[:].rearrange("p t (c i) -> p c t i", i=4)
+        nc.vector.tensor_copy(z_dst[:, 0:64], z_src[:, 0:64])
+        nc.scalar.copy(z_dst[:, 64:128], z_src[:, 64:128])
+        for half in range(2):
+            nc.vector.quantize_mx(out=z_words[:, cols(half)].bitcast(FP8X4), scales=z_scales[:, cols(half)],
+                                  in_=z_il[:, half * HALF * PACK : (half + 1) * HALF * PACK])
+            if half == 0:
+                nc.vector.quantize_mx(out=w_words[:].bitcast(FP8X4), scales=w_scales[:], in_=w_il[:])
+
+        h_banks = product(["b5", "b6", "b7", "b0", "b1"], w_words, w_scales, z_words, z_scales)
+
+        out_rows = out.rearrange("(p t) j -> p t j", t=PACK)
+        for t in range(PACK):
+            h_sb = keep.tile([P, S], F32, name="h_sb%d" % t)
+            hop = keep.tile([P, S], F32, name="hop%d" % t)
+            st = keep.tile([P, S], F32, name="st%d" % t)
+            sent = keep.tile([P, S], F32, name="sent%d" % t)
+            res = keep.tile([P, S], F32, name="res%d" % t)
+            if t == 0:
+                nc.scalar.copy(h_sb[:, cols(0)], h_banks[0][:])
+                nc.vector.tensor_copy(h_sb[:, cols(1)], h_banks[1][:])
+            else:
+                nc.scalar.copy(h_sb[:], h_banks[t + 1][:])
+            pieces = ((0, 128), (128, 256), (256, 512)) if t == 0 else ((0, 256), (256, 512))
+            for lo, hi in pieces:
+                nc.scalar.activation(hop[:, lo:hi], h_sb[:].indirect(n3_t[:, lo // 16 : hi // 16]), ACT.Copy)
+            if t > 0:
+                nc.vector.tensor_tensor(st[:], hop[:], h_banks[t + 1][:], ALU.max)
+            for lo, hi in pieces:
+                if t == 0:
+                    nc.vector.tensor_tensor(st[:, lo:hi], hop[:, lo:hi], h_banks[lo // HALF][:, lo % HALF : lo % HALF + hi - lo], ALU.max)
+                nc.vector.tensor_copy(sent[:].indirect(n4_t[:, lo // 16 : hi // 16]), st[:, lo:hi])
+            if t + 1 < PACK:
+                nc.gpsimd.tensor_tensor(res[:], sent[:], h_sb[:], ALU.subtract)
+                nc.sync.dma_start(out_rows[:, t, :], res[:])
+            else:
+                for half, queue in enumerate((nc.sync, nc.scalar)):
+                    nc.vector.tensor_tensor(res[:, cols(half)], sent[:, cols(half)], h_banks[t + 1][:, cols(half)], ALU.subtract)
+                    queue.dma_start(out_rows[:, t, cols(half)], res[:, cols(half)])

@@ -45,6 +45,11 @@ def tile_picked_hwlratiosendhop_none_p_kernel(tc, x_words, x_scales, d_words, d_
         nc.gpsimd.memset(xs_tab[:].bitcast(I32), 0)
         nc.vector.memset(ds_tab[:].bitcast(I32), 0)
 
+        warm_in = keep.tile([P, 1], F32, name="warm_in")
+        warm_out = keep.tile([P, 1], F32, name="warm_out")
+        nc.vector.memset(warm_in[:], 1.0)
+        nc.scalar.activation(warm_out[:], warm_in[:], ACT.Abs_reciprocal_sqrt, bias=0.5)
+
         offs_t = load_list("offs_t", offs)
         ci_t = load_list("ci_t", ci)
         n2_t = load_list("n2_t", n2)

@@ -17,6 +17,7 @@ PACK = 4
 TABLE = 2048
 S = 512
 HALF = 256
+SPLIT = 336
 FLOPS = 2 * 2 * 512 * 512 * 512
 
 
@@ -63,8 +64,6 @@ def tile_picked_hwlratiosendhop_none_p_kernel(tc, x_words, x_scales, d_words, d_
         for j in range(4):
             nc.scalar.dma_start(ds_tab[:].bitcast(I32)[j:P:32, :], d_scales[0].bitcast(I32)[j:16:4, :])
         nc.sync.dma_start(xw_tab[:].bitcast(I32), x_words[0].rearrange("p c r -> p (c r)").bitcast(I32))
-        gain = keep.tile([P, PACK], F32, name="gain")
-        nc.gpsimd.dma_start(gain[:], gn.rearrange("(p t) o -> p (t o)", t=PACK))
 
         xs_pick = keep.tile([P, S], U8, name="xs_pick")
         xs_plane = keep.tile([P, S], U8, name="xs_plane", align_bytes=64)
@@ -72,6 +71,8 @@ def tile_picked_hwlratiosendhop_none_p_kernel(tc, x_words, x_scales, d_words, d_
         nc.vector.tensor_copy(xs_plane[:].bitcast(I32), xs_pick[:].bitcast(I32))
         for j in range(1, 4):
             nc.scalar.dma_start(xs_plane[:].bitcast(I32)[j:P:32, :], xs_pick[:].bitcast(I32)[8 * j : P : 32, :])
+        gain = keep.tile([P, PACK], F32, name="gain", tag="xs_tab")
+        nc.gpsimd.dma_start(gain[:], gn.rearrange("(p t) o -> p (t o)", t=PACK))
         ds_pick = keep.tile([P, S], U8, name="ds_pick", align_bytes=64)
         nc.vector.tensor_copy(ds_pick[:].rearrange("p (t m) -> p m t", t=PACK), ds_tab[:].indirect(ci_t[:]))
         dw_pick = keep.tile([P, S], U32, name="dw_pick", align_bytes=64)
@@ -82,110 +83,157 @@ def tile_picked_hwlratiosendhop_none_p_kernel(tc, x_words, x_scales, d_words, d_
         for half in range(2):
             nc.vector.tensor_copy(xw_pick[:, cols(half)], xw_tab[:].indirect(offs_t[:, entries(half)]))
 
-        def product(bank_names, lhs_words, lhs_scales, rhs_words, rhs_scales):
-            banks = []
-            for half in range(2):
-                bank = psum.tile([P, HALF], F32, name=bank_names[half])
-                nc.tensor.matmul_mx(out=bank[:], lhsT=lhs_words[:, rows(0)].bitcast(FP8X4), lhsT_scale=lhs_scales[:, rows(0)],
-                                    rhs=rhs_words[:, cols(half)].bitcast(FP8X4), rhs_scale=rhs_scales[:, cols(half)], start=True, stop=True)
-                banks.append(bank)
-            for t in range(1, PACK):
-                bank = psum.tile([P, S], F32, name=bank_names[t + 1])
-                nc.tensor.matmul_mx(out=bank[:], lhsT=lhs_words[:, rows(t)].bitcast(FP8X4), lhsT_scale=lhs_scales[:, rows(t)],
-                                    rhs=rhs_words[:].bitcast(FP8X4), rhs_scale=rhs_scales[:], start=True, stop=True)
-                banks.append(bank)
-            return banks
+        def first_tile(bank_name, half, lhs, rhs_words, rhs_scales):
+            bank = psum.tile([P, HALF], F32, name=bank_name)
+            nc.tensor.matmul_mx(out=bank[:], lhsT=lhs[0].bitcast(FP8X4), lhsT_scale=lhs[1],
+                                rhs=rhs_words[:, cols(half)].bitcast(FP8X4), rhs_scale=rhs_scales[:, cols(half)], start=True, stop=True)
+            return bank
 
-        s_banks = product(["b0", "b1", "b2", "b3", "b4"], dw_pick, ds_pick, xw_pick, xs_plane)
+        def whole_tile(bank_name, lhs, rhs_words, rhs_scales):
+            bank = psum.tile([P, S], F32, name=bank_name)
+            nc.tensor.matmul_mx(out=bank[:], lhsT=lhs[0].bitcast(FP8X4), lhsT_scale=lhs[1],
+                                rhs=rhs_words[:].bitcast(FP8X4), rhs_scale=rhs_scales[:], start=True, stop=True)
+            return bank
+
+        d_lhs = [(dw_pick[:, rows(t)], ds_pick[:, rows(t)]) for t in range(PACK)]
 
         def halves(name):
             return [keep.tile([P, HALF], F32, name="%s%d" % (name, t)) for t in range(PACK)]
 
         s_sb = [keep.tile([P, S], F32, name="s_sb%d" % t) for t in range(PACK)]
         pa, pb, size, root, recip = halves("pa"), halves("pb"), halves("size"), halves("root"), halves("recip")
-        nc.scalar.activation(s_sb[0][:, cols(0)], s_banks[0][:], ACT.Copy, scale=0.0625)
-        nc.vector.tensor_scalar_mul(s_sb[0][:, cols(1)], s_banks[1][:], 0.0625)
+        left = first_tile("bank0", 0, d_lhs[0], xw_pick, xs_plane)
+        right = first_tile("bank1", 1, d_lhs[0], xw_pick, xs_plane)
+        nc.scalar.activation(s_sb[0][:, cols(0)], left[:], ACT.Copy, scale=0.0625)
+        nc.vector.tensor_scalar_mul(s_sb[0][:, cols(1)], right[:], 0.0625)
+        s_banks = [None] + [whole_tile("bank%d" % t, d_lhs[t], xw_pick, xs_plane) for t in range(1, PACK)]
         nc.vector.tensor_copy(pa[0][:], s_sb[0][:].indirect(n1_t[:]))
         nc.scalar.activation(pb[0][:], s_sb[0][:].indirect(n2_t[:]), ACT.Copy)
-        for t in range(PACK):
-            ahead = t + 1 < PACK
-            if ahead:
-                nc.scalar.activation(s_sb[t + 1][:], s_banks[t + 2][:], ACT.Copy, scale=0.0625)
+
+        def leave_bank(t):
+            nc.scalar.activation(s_sb[t][:], s_banks[t][:], ACT.Copy, scale=0.0625)
+
+        def fetch_pair(dst, t, listed):
+            nc.scalar.activation(dst[t][:], s_sb[t][:].indirect(listed[:]), ACT.Copy)
+
+        def take_size(t):
             nc.scalar.activation(size[t][:], pb[t][:], ACT.Abs)
-            if ahead:
-                nc.scalar.activation(pb[t + 1][:], s_sb[t + 1][:].indirect(n2_t[:]), ACT.Copy)
+
+        def take_root(t):
             nc.scalar.activation(root[t][:], size[t][:], ACT.Abs_reciprocal_sqrt, bias=0.5)
-            if ahead:
-                nc.scalar.activation(pa[t + 1][:], s_sb[t + 1][:].indirect(n1_t[:]), ACT.Copy)
+
+        def take_square(t):
             nc.scalar.activation(recip[t][:], root[t][:], ACT.Square)
+
+        leave_bank(1)
+        take_size(0)
+        fetch_pair(pb, 1, n2_t)
+        fetch_pair(pa, 1, n1_t)
+        for t in (2, 3):
+            leave_bank(t)
+            if t == 3:
+                take_size(1)
+            else:
+                take_root(0)
+            fetch_pair(pb, t, n2_t)
+            if t == 3:
+                take_root(1)
+            fetch_pair(pa, t, n1_t)
+            take_square(t - 2)
+        for step in (take_size, take_root, take_square):
+            for t in (2, 3):
+                step(t)
 
         z_planes = keep.tile([P, PACK, S], BF16, name="z_planes")
         larger = halves("larger")
         placed = [keep.tile([P, S], F32, name="placed%d" % t, align_bytes=64) for t in range(PACK)]
-        w_src = w_raw[:].rearrange("p j (m t) -> p m j t", t=PACK)
 
-        def weave_w1(w_il, quarters):
-            w_dst = w_il[:].rearrange("p (t m j) -> p m j t", t=PACK, j=PACK)
-            for q in quarters:
-                nc.scalar.copy(w_dst[:, 32 * q : 32 * q + 32], w_src[:, 32 * q : 32 * q + 32])
+        def take_larger(t):
+            nc.vector.tensor_tensor(larger[t][:], pa[t][:], pb[t][:], ALU.max)
 
-        nc.vector.tensor_tensor(larger[0][:], pa[0][:], pb[0][:], ALU.max)
-        for t in range(PACK):
+        def put_larger(t):
             nc.vector.tensor_copy(placed[t][:].indirect(n2_t[:]), larger[t][:])
-            if t + 1 < PACK:
-                nc.vector.tensor_tensor(larger[t + 1][:], pa[t + 1][:], pb[t + 1][:], ALU.max)
+
+        def put_ratio(t):
             nc.vector.tensor_tensor(placed[t][:].indirect(n1_t[:]), pa[t][:], recip[t][:], ALU.mult)
-            if t == 2:
-                w_il = keep.tile([P, PACK * S], BF16, name="w_il", tag="placed1", align_bytes=64)
-                weave_w1(w_il, (0, 1))
-            if t + 1 < PACK:
-                nc.scalar.activation(z_planes[:, t, :], placed[t][:], ACT.Copy, scale=gain[:, t : t + 1])
-            else:
-                nc.vector.tensor_scalar_mul(z_planes[:, t, :], placed[t][:], gain[:, t : t + 1])
-        weave_w1(w_il, (2, 3))
+
+        def round_plane(t, lo, hi):
+            nc.scalar.activation(z_planes[:, t, lo:hi], placed[t][:, lo:hi], ACT.Copy, scale=gain[:, t : t + 1])
+
+        for t in (0, 1):
+            take_larger(t)
+            put_larger(t)
+        for t in (2, 3):
+            take_larger(t)
+            put_ratio(t - 2)
+            put_larger(t)
+        put_ratio(2)
+        put_ratio(3)
+
+        round_plane(0, 0, S)
+        w_il = keep.tile([P, PACK * S], BF16, name="w_il", tag="placed0", align_bytes=64)
+        w_dst = w_il[:].rearrange("p (t m j) -> p m j t", t=PACK, j=PACK)
+        w_src = w_raw[:].rearrange("p j (m t) -> p m j t", t=PACK)
+        nc.scalar.copy(w_dst, w_src)
+        w0_words = keep.tile([P, P], U32, name="w0_words", align_bytes=64)
+        w0_scales = keep.tile([P, P], U8, name="w0_scales", align_bytes=64)
+        nc.vector.quantize_mx(out=w0_words[:].bitcast(FP8X4), scales=w0_scales[:], in_=w_il[:, 0 : P * PACK])
+        round_plane(1, 0, S)
+        round_plane(2, 0, S)
+        nc.vector.tensor_scalar_mul(z_planes[:, 3, 0:SPLIT], placed[3][:, 0:SPLIT], gain[:, 3:4])
+        round_plane(3, SPLIT, S)
 
         z_il = keep.tile([P, S * PACK], BF16, name="z_il", align_bytes=64)
         z_words = keep.tile([P, S], U32, name="z_words", align_bytes=64)
         z_scales = keep.tile([P, S], U8, name="z_scales", align_bytes=64)
-        w_words = keep.tile([P, S], U32, name="w_words", align_bytes=64)
-        w_scales = keep.tile([P, S], U8, name="w_scales", align_bytes=64)
         z_dst = z_il[:].rearrange("p (c i t) -> p c t i", i=4, t=PACK)
         z_src = z_planes[:].rearrange("p t (c i) -> p c t i", i=4)
-        nc.vector.tensor_copy(z_dst[:, 0:64], z_src[:, 0:64])
-        nc.scalar.copy(z_dst[:, 64:128], z_src[:, 64:128])
+        nc.vector.tensor_copy(z_dst[:, 0 : SPLIT // 4], z_src[:, 0 : SPLIT // 4])
+        nc.scalar.copy(z_dst[:, SPLIT // 4 : S // 4], z_src[:, SPLIT // 4 : S // 4])
         for half in range(2):
             nc.vector.quantize_mx(out=z_words[:, cols(half)].bitcast(FP8X4), scales=z_scales[:, cols(half)],
                                   in_=z_il[:, half * HALF * PACK : (half + 1) * HALF * PACK])
-            if half == 0:
-                nc.vector.quantize_mx(out=w_words[:].bitcast(FP8X4), scales=w_scales[:], in_=w_il[:])
+        wr_words = keep.tile([P, S - P], U32, name="wr_words", tag="z_il", align_bytes=64)
+        wr_scales = keep.tile([P, S - P], U8, name="wr_scales", align_bytes=64)
+        nc.vector.quantize_mx(out=wr_words[:].bitcast(FP8X4), scales=wr_scales[:], in_=w_il[:, P * PACK : S * PACK])
+        w_lhs = [(w0_words[:], w0_scales[:])] + [(wr_words[:, rows(t)], wr_scales[:, rows(t)]) for t in range(PACK - 1)]
 
-        h_banks = product(["b5", "b6", "b7", "b0", "b1"], w_words, w_scales, z_words, z_scales)
+        h_sbs = [keep.tile([P, S], F32, name="h_sb%d" % t) for t in range(PACK)]
+        first = [first_tile("bank%d" % (4 + half), half, w_lhs[0], z_words, z_scales) for half in range(2)]
+        for half in range(2):
+            nc.scalar.copy(h_sbs[0][:, cols(half)], first[half][:])
+        h_banks = [None] + [whole_tile("bank%d" % (4 + t), w_lhs[t], z_words, z_scales) for t in range(1, PACK)]
 
         out_rows = out.rearrange("(p t) j -> p t j", t=PACK)
-        for t in range(PACK):
-            h_sb = keep.tile([P, S], F32, name="h_sb%d" % t)
-            hop = keep.tile([P, S], F32, name="hop%d" % t)
-            st = keep.tile([P, S], F32, name="st%d" % t)
-            sent = keep.tile([P, S], F32, name="sent%d" % t)
-            res = keep.tile([P, S], F32, name="res%d" % t)
-            if t == 0:
-                nc.scalar.copy(h_sb[:, cols(0)], h_banks[0][:])
-                nc.vector.tensor_copy(h_sb[:, cols(1)], h_banks[1][:])
-            else:
-                nc.scalar.copy(h_sb[:], h_banks[t + 1][:])
-            pieces = ((0, 128), (128, 256), (256, 512)) if t == 0 else ((0, 256), (256, 512))
-            for lo, hi in pieces:
-                nc.scalar.activation(hop[:, lo:hi], h_sb[:].indirect(n3_t[:, lo // 16 : hi // 16]), ACT.Copy)
-            if t > 0:
-                nc.vector.tensor_tensor(st[:], hop[:], h_banks[t + 1][:], ALU.max)
-            for lo, hi in pieces:
-                if t == 0:
-                    nc.vector.tensor_tensor(st[:, lo:hi], hop[:, lo:hi], h_banks[lo // HALF][:, lo % HALF : lo % HALF + hi - lo], ALU.max)
-                nc.vector.tensor_copy(sent[:].indirect(n4_t[:, lo // 16 : hi // 16]), st[:, lo:hi])
-            if t + 1 < PACK:
-                nc.gpsimd.tensor_tensor(res[:], sent[:], h_sb[:], ALU.subtract)
-                nc.sync.dma_start(out_rows[:, t, :], res[:])
-            else:
-                for half, queue in enumerate((nc.sync, nc.scalar)):
-                    nc.vector.tensor_tensor(res[:, cols(half)], sent[:, cols(half)], h_banks[t + 1][:, cols(half)], ALU.subtract)
-                    queue.dma_start(out_rows[:, t, cols(half)], res[:, cols(half)])
+        hop = [keep.tile([P, S], F32, name="hop%d" % t) for t in range(PACK)]
+        st = [keep.tile([P, S], F32, name="st%d" % t) for t in range(PACK)]
+        sent = [keep.tile([P, 2 * S], F32, name="sent%d" % t) for t in range(PACK)]
+        res = [keep.tile([P, S], F32, name="res%d" % t) for t in range(PACK)]
+
+        def fetch(t, lo, hi):
+            nc.scalar.activation(hop[t][:, lo:hi], h_sbs[t][:].indirect(n3_t[:, lo // 16 : hi // 16]), ACT.Copy)
+
+        def send(t, lo, hi):
+            nc.vector.tensor_copy(sent[t][:].indirect(n4_t[:, lo // 16 : hi // 16]), st[t][:, lo:hi])
+
+        pieces = ((0, 128), (128, 256), (256, 512))
+        for lo, hi in pieces:
+            fetch(0, lo, hi)
+        for t in range(1, PACK):
+            nc.scalar.copy(h_sbs[t][:], h_banks[t][:])
+            fetch(t, 0, HALF)
+            fetch(t, HALF, S)
+        for k, (lo, hi) in enumerate(pieces):
+            nc.vector.tensor_tensor(st[0][:, lo:hi], hop[0][:, lo:hi], h_sbs[0][:, lo:hi], ALU.max)
+            if k > 0:
+                send(0, *pieces[k - 1])
+        send(0, *pieces[-1])
+        for t in range(1, PACK):
+            nc.vector.tensor_tensor(st[t][:], hop[t][:], h_banks[t][:], ALU.max)
+            nc.vector.tensor_tensor(res[t - 1][:], sent[t - 1][:, 0:S], h_sbs[t - 1][:], ALU.subtract)
+            nc.sync.dma_start(out_rows[:, t - 1, :], res[t - 1][:])
+            send(t, 0, S)
+        last = PACK - 1
+        for half, queue in enumerate((nc.sync, nc.scalar)):
+            nc.vector.tensor_tensor(res[last][:, cols(half)], sent[last][:, cols(half)], h_banks[last][:, cols(half)], ALU.subtract)
+            queue.dma_start(out_rows[:, last, cols(half)], res[last][:, cols(half)])

@@ -44,7 +44,7 @@ def tile_picked_hwlratiosendhop_none_p_kernel(tc, x_words, x_scales, d_words, d_
         xs_tab = keep.tile([P, TABLE], U8, name="xs_tab")
         ds_tab = keep.tile([P, TABLE], U8, name="ds_tab")
         nc.gpsimd.memset(xs_tab[:].bitcast(I32), 0)
-        nc.vector.memset(ds_tab[:].bitcast(I32), 0)
+        nc.gpsimd.memset(ds_tab[:].bitcast(I32), 0)
 
         warm_in = keep.tile([P, 1], F32, name="warm_in")
         warm_out = keep.tile([P, 1], F32, name="warm_out")
@@ -55,7 +55,7 @@ def tile_picked_hwlratiosendhop_none_p_kernel(tc, x_words, x_scales, d_words, d_
         ci_t = load_list("ci_t", ci)
         n2_t = load_list("n2_t", n2)
         n1_t = load_list("n1_t", n1)
-        nc.gpsimd.dma_start(xs_tab[:].bitcast(I32)[0:P:8, :], x_scales[0].bitcast(I32))
+        nc.scalar.dma_start(xs_tab[:].bitcast(I32)[0:P:8, :], x_scales[0].bitcast(I32))
         dw_tab = keep.tile([P, TABLE], U32, name="dw_tab", tag="dict_then_w1")
         xw_tab = keep.tile([P, TABLE], U32, name="xw_tab")
         nc.sync.dma_start(dw_tab[:].bitcast(I32), d_words[0].rearrange("p c r -> p (c r)").bitcast(I32))
@@ -63,7 +63,7 @@ def tile_picked_hwlratiosendhop_none_p_kernel(tc, x_words, x_scales, d_words, d_
         n4_t = load_list("n4_t", n4)
         for j in range(4):
             nc.scalar.dma_start(ds_tab[:].bitcast(I32)[j:P:32, :], d_scales[0].bitcast(I32)[j:16:4, :])
-        nc.sync.dma_start(xw_tab[:].bitcast(I32), x_words[0].rearrange("p c r -> p (c r)").bitcast(I32))
+        nc.gpsimd.dma_start(xw_tab[:].bitcast(I32), x_words[0].rearrange("p c r -> p (c r)").bitcast(I32))
 
         xs_pick = keep.tile([P, S], U8, name="xs_pick")
         xs_plane = keep.tile([P, S], U8, name="xs_plane", align_bytes=64)
@@ -230,7 +230,7 @@ def tile_picked_hwlratiosendhop_none_p_kernel(tc, x_words, x_scales, d_words, d_
         send(0, *pieces[-1])
         for t in range(1, PACK):
             nc.vector.tensor_tensor(st[t][:], hop[t][:], h_banks[t][:], ALU.max)
-            nc.vector.tensor_tensor(res[t - 1][:], sent[t - 1][:, 0:S], h_sbs[t - 1][:], ALU.subtract)
+            nc.gpsimd.tensor_tensor(res[t - 1][:], sent[t - 1][:, 0:S], h_sbs[t - 1][:], ALU.subtract)
             nc.sync.dma_start(out_rows[:, t - 1, :], res[t - 1][:])
             send(t, 0, S)
         last = PACK - 1

@@ -17,7 +17,10 @@ PACK = 4
 TABLE = 2048
 S = 512
 HALF = 256
-SPLIT = 336
+LANES = 16
+QUAD = 32
+RUN = 4
+VECTOR_COLS = 336
 FLOPS = 2 * 2 * 512 * 512 * 512
 
 
@@ -25,6 +28,7 @@ def tile_picked_hwlratiosendhop_none_p_kernel(tc, x_words, x_scales, d_words, d_
     nc = tc.nc
     with ExitStack() as ctx:
         keep = ctx.enter_context(tc.tile_pool(name="keep", bufs=1))
+        shared = ctx.enter_context(tc.tile_pool(name="shared", bufs=1))
         psum = ctx.enter_context(tc.psum_pool(name="psum", bufs=1))
 
         def load_list(name, src):
@@ -35,14 +39,17 @@ def tile_picked_hwlratiosendhop_none_p_kernel(tc, x_words, x_scales, d_words, d_
         def cols(half):
             return slice(half * HALF, (half + 1) * HALF)
 
-        def entries(half):
-            return slice(half * HALF // 16, (half + 1) * HALF // 16)
+        def entries(lo, hi):
+            return slice(lo // LANES, hi // LANES)
 
         def rows(t):
             return slice(t * P, (t + 1) * P)
 
+        def row_tiles(name, width, **placing):
+            return [keep.tile([P, width], F32, name="%s%d" % (name, t), **placing) for t in range(PACK)]
+
         xs_tab = keep.tile([P, TABLE], U8, name="xs_tab")
-        ds_tab = keep.tile([P, TABLE], U8, name="ds_tab")
+        ds_tab = shared.tile([P, TABLE], U8, name="ds_tab", offset=0)
         nc.gpsimd.memset(xs_tab[:].bitcast(I32), 0)
         nc.gpsimd.memset(ds_tab[:].bitcast(I32), 0)
 
@@ -56,65 +63,56 @@ def tile_picked_hwlratiosendhop_none_p_kernel(tc, x_words, x_scales, d_words, d_
         n2_t = load_list("n2_t", n2)
         n1_t = load_list("n1_t", n1)
         nc.scalar.dma_start(xs_tab[:].bitcast(I32)[0:P:8, :], x_scales[0].bitcast(I32))
-        dw_tab = keep.tile([P, TABLE], U32, name="dw_tab", tag="dict_then_w1")
+        dw_tab = shared.tile([P, TABLE], U32, name="dw_tab", offset=TABLE)
         xw_tab = keep.tile([P, TABLE], U32, name="xw_tab")
         nc.sync.dma_start(dw_tab[:].bitcast(I32), d_words[0].rearrange("p c r -> p (c r)").bitcast(I32))
         n3_t = load_list("n3_t", n3)
         n4_t = load_list("n4_t", n4)
-        for j in range(4):
-            nc.scalar.dma_start(ds_tab[:].bitcast(I32)[j:P:32, :], d_scales[0].bitcast(I32)[j:16:4, :])
+        for j in range(PACK):
+            nc.scalar.dma_start(ds_tab[:].bitcast(I32)[j:P:QUAD, :], d_scales[0].bitcast(I32)[j:16:PACK, :])
         nc.gpsimd.dma_start(xw_tab[:].bitcast(I32), x_words[0].rearrange("p c r -> p (c r)").bitcast(I32))
 
         xs_pick = keep.tile([P, S], U8, name="xs_pick")
         xs_plane = keep.tile([P, S], U8, name="xs_plane", align_bytes=64)
+        nc.gpsimd.memset(xs_plane[:].bitcast(I32), 0)
         nc.vector.tensor_copy(xs_pick[:], xs_tab[:].indirect(offs_t[:]))
-        nc.vector.tensor_copy(xs_plane[:].bitcast(I32), xs_pick[:].bitcast(I32))
-        for j in range(1, 4):
-            nc.scalar.dma_start(xs_plane[:].bitcast(I32)[j:P:32, :], xs_pick[:].bitcast(I32)[8 * j : P : 32, :])
+        for j in range(PACK):
+            nc.scalar.dma_start(xs_plane[:].bitcast(I32)[j:P:QUAD, :], xs_pick[:].bitcast(I32)[8 * j : P : QUAD, :])
         gain = keep.tile([P, PACK], F32, name="gain", tag="xs_tab")
         nc.gpsimd.dma_start(gain[:], gn.rearrange("(p t) o -> p (t o)", t=PACK))
-        ds_pick = keep.tile([P, S], U8, name="ds_pick", align_bytes=64)
-        nc.vector.tensor_copy(ds_pick[:].rearrange("p (t m) -> p m t", t=PACK), ds_tab[:].indirect(ci_t[:]))
         dw_pick = keep.tile([P, S], U32, name="dw_pick", align_bytes=64)
         nc.vector.tensor_copy(dw_pick[:].rearrange("p (t m) -> p m t", t=PACK), dw_tab[:].indirect(ci_t[:]))
-        w_raw = keep.tile([P, PACK, S], F32, name="w_raw", tag="dict_then_w1")
-        nc.sync.dma_start(w_raw[:], w1.rearrange("(p j) n -> p j n", j=PACK))
-        xw_pick = keep.tile([P, S], U32, name="xw_pick", align_bytes=64)
+        ds_pick = keep.tile([P, S], U8, name="ds_pick", align_bytes=64)
+        nc.vector.tensor_copy(ds_pick[:].rearrange("p (t m) -> p m t", t=PACK), ds_tab[:].indirect(ci_t[:]))
+        xw_pick = shared.tile([P, S], U32, name="xw_pick", offset=TABLE // 2, align_bytes=64)
         for half in range(2):
-            nc.vector.tensor_copy(xw_pick[:, cols(half)], xw_tab[:].indirect(offs_t[:, entries(half)]))
+            nc.vector.tensor_copy(xw_pick[:, cols(half)], xw_tab[:].indirect(offs_t[:, entries(half * HALF, (half + 1) * HALF)]))
 
-        def first_tile(bank_name, half, lhs, rhs_words, rhs_scales):
-            bank = psum.tile([P, HALF], F32, name=bank_name)
-            nc.tensor.matmul_mx(out=bank[:], lhsT=lhs[0].bitcast(FP8X4), lhsT_scale=lhs[1],
-                                rhs=rhs_words[:, cols(half)].bitcast(FP8X4), rhs_scale=rhs_scales[:, cols(half)], start=True, stop=True)
-            return bank
+        w_raw = keep.tile([P, PACK, S], F32, name="w_raw", tag="xw_tab")
+        nc.sync.dma_start(w_raw[:], w1.rearrange("(p j) n -> p j n", j=PACK))
 
-        def whole_tile(bank_name, lhs, rhs_words, rhs_scales):
-            bank = psum.tile([P, S], F32, name=bank_name)
+        def product(bank_name, lhs, rhs_words, rhs_scales, columns):
+            bank = psum.tile([P, columns.stop - columns.start], F32, name=bank_name)
             nc.tensor.matmul_mx(out=bank[:], lhsT=lhs[0].bitcast(FP8X4), lhsT_scale=lhs[1],
-                                rhs=rhs_words[:].bitcast(FP8X4), rhs_scale=rhs_scales[:], start=True, stop=True)
+                                rhs=rhs_words[:, columns].bitcast(FP8X4), rhs_scale=rhs_scales[:, columns], start=True, stop=True)
             return bank
 
         d_lhs = [(dw_pick[:, rows(t)], ds_pick[:, rows(t)]) for t in range(PACK)]
-
-        def halves(name):
-            return [keep.tile([P, HALF], F32, name="%s%d" % (name, t)) for t in range(PACK)]
-
-        s_sb = [keep.tile([P, S], F32, name="s_sb%d" % t) for t in range(PACK)]
-        pa, pb, size, root, recip = halves("pa"), halves("pb"), halves("size"), halves("root"), halves("recip")
-        left = first_tile("bank0", 0, d_lhs[0], xw_pick, xs_plane)
-        right = first_tile("bank1", 1, d_lhs[0], xw_pick, xs_plane)
+        s_sb = row_tiles("s_sb", S)
+        pa, pb, size, root, recip = [row_tiles(name, HALF) for name in ("pa", "pb", "size", "root", "recip")]
+        left = product("bank0", d_lhs[0], xw_pick, xs_plane, cols(0))
+        right = product("bank1", d_lhs[0], xw_pick, xs_plane, cols(1))
         nc.scalar.activation(s_sb[0][:, cols(0)], left[:], ACT.Copy, scale=0.0625)
         nc.vector.tensor_scalar_mul(s_sb[0][:, cols(1)], right[:], 0.0625)
-        s_banks = [None] + [whole_tile("bank%d" % t, d_lhs[t], xw_pick, xs_plane) for t in range(1, PACK)]
+        s_banks = {t: product("bank%d" % t, d_lhs[t], xw_pick, xs_plane, slice(0, S)) for t in range(1, PACK)}
         nc.vector.tensor_copy(pa[0][:], s_sb[0][:].indirect(n1_t[:]))
         nc.scalar.activation(pb[0][:], s_sb[0][:].indirect(n2_t[:]), ACT.Copy)
 
         def leave_bank(t):
             nc.scalar.activation(s_sb[t][:], s_banks[t][:], ACT.Copy, scale=0.0625)
 
-        def fetch_pair(dst, t, listed):
-            nc.scalar.activation(dst[t][:], s_sb[t][:].indirect(listed[:]), ACT.Copy)
+        def fetch_pair(dst, t, list_tile):
+            nc.scalar.activation(dst[t][:], s_sb[t][:].indirect(list_tile[:]), ACT.Copy)
 
         def take_size(t):
             nc.scalar.activation(size[t][:], pb[t][:], ACT.Abs)
@@ -129,24 +127,27 @@ def tile_picked_hwlratiosendhop_none_p_kernel(tc, x_words, x_scales, d_words, d_
         take_size(0)
         fetch_pair(pb, 1, n2_t)
         fetch_pair(pa, 1, n1_t)
-        for t in (2, 3):
-            leave_bank(t)
-            if t == 3:
-                take_size(1)
-            else:
-                take_root(0)
-            fetch_pair(pb, t, n2_t)
-            if t == 3:
-                take_root(1)
-            fetch_pair(pa, t, n1_t)
-            take_square(t - 2)
+
+        leave_bank(2)
+        take_root(0)
+        fetch_pair(pb, 2, n2_t)
+        fetch_pair(pa, 2, n1_t)
+        take_square(0)
+
+        leave_bank(3)
+        take_size(1)
+        fetch_pair(pb, 3, n2_t)
+        take_root(1)
+        fetch_pair(pa, 3, n1_t)
+        take_square(1)
+
         for step in (take_size, take_root, take_square):
             for t in (2, 3):
                 step(t)
 
         z_planes = keep.tile([P, PACK, S], BF16, name="z_planes")
-        larger = halves("larger")
-        placed = [keep.tile([P, S], F32, name="placed%d" % t, align_bytes=64) for t in range(PACK)]
+        larger = row_tiles("larger", HALF)
+        placed = row_tiles("placed", S, align_bytes=64)
 
         def take_larger(t):
             nc.vector.tensor_tensor(larger[t][:], pa[t][:], pb[t][:], ALU.max)
@@ -172,24 +173,22 @@ def tile_picked_hwlratiosendhop_none_p_kernel(tc, x_words, x_scales, d_words, d_
 
         round_plane(0, 0, S)
         w_il = keep.tile([P, PACK * S], BF16, name="w_il", tag="placed0", align_bytes=64)
-        w_dst = w_il[:].rearrange("p (t m j) -> p m j t", t=PACK, j=PACK)
-        w_src = w_raw[:].rearrange("p j (m t) -> p m j t", t=PACK)
-        nc.scalar.copy(w_dst, w_src)
+        nc.scalar.copy(w_il[:].rearrange("p (t m j) -> p m j t", t=PACK, j=PACK), w_raw[:].rearrange("p j (m t) -> p m j t", t=PACK))
         w0_words = keep.tile([P, P], U32, name="w0_words", align_bytes=64)
         w0_scales = keep.tile([P, P], U8, name="w0_scales", align_bytes=64)
         nc.vector.quantize_mx(out=w0_words[:].bitcast(FP8X4), scales=w0_scales[:], in_=w_il[:, 0 : P * PACK])
         round_plane(1, 0, S)
         round_plane(2, 0, S)
-        nc.vector.tensor_scalar_mul(z_planes[:, 3, 0:SPLIT], placed[3][:, 0:SPLIT], gain[:, 3:4])
-        round_plane(3, SPLIT, S)
+        nc.vector.tensor_scalar_mul(z_planes[:, 3, 0:VECTOR_COLS], placed[3][:, 0:VECTOR_COLS], gain[:, 3:4])
+        round_plane(3, VECTOR_COLS, S)
 
         z_il = keep.tile([P, S * PACK], BF16, name="z_il", align_bytes=64)
         z_words = keep.tile([P, S], U32, name="z_words", align_bytes=64)
         z_scales = keep.tile([P, S], U8, name="z_scales", align_bytes=64)
-        z_dst = z_il[:].rearrange("p (c i t) -> p c t i", i=4, t=PACK)
-        z_src = z_planes[:].rearrange("p t (c i) -> p c t i", i=4)
-        nc.vector.tensor_copy(z_dst[:, 0 : SPLIT // 4], z_src[:, 0 : SPLIT // 4])
-        nc.scalar.copy(z_dst[:, SPLIT // 4 : S // 4], z_src[:, SPLIT // 4 : S // 4])
+        z_dst = z_il[:].rearrange("p (c i t) -> p c t i", i=RUN, t=PACK)
+        z_src = z_planes[:].rearrange("p t (c i) -> p c t i", i=RUN)
+        nc.vector.tensor_copy(z_dst[:, 0 : VECTOR_COLS // RUN], z_src[:, 0 : VECTOR_COLS // RUN])
+        nc.scalar.copy(z_dst[:, VECTOR_COLS // RUN : S // RUN], z_src[:, VECTOR_COLS // RUN : S // RUN])
         for half in range(2):
             nc.vector.quantize_mx(out=z_words[:, cols(half)].bitcast(FP8X4), scales=z_scales[:, cols(half)],
                                   in_=z_il[:, half * HALF * PACK : (half + 1) * HALF * PACK])
@@ -198,42 +197,45 @@ def tile_picked_hwlratiosendhop_none_p_kernel(tc, x_words, x_scales, d_words, d_
         nc.vector.quantize_mx(out=wr_words[:].bitcast(FP8X4), scales=wr_scales[:], in_=w_il[:, P * PACK : S * PACK])
         w_lhs = [(w0_words[:], w0_scales[:])] + [(wr_words[:, rows(t)], wr_scales[:, rows(t)]) for t in range(PACK - 1)]
 
-        h_sbs = [keep.tile([P, S], F32, name="h_sb%d" % t) for t in range(PACK)]
-        first = [first_tile("bank%d" % (4 + half), half, w_lhs[0], z_words, z_scales) for half in range(2)]
+        h_sb = row_tiles("h_sb", S)
+        first = [product("bank%d" % (PACK + half), w_lhs[0], z_words, z_scales, cols(half)) for half in range(2)]
         for half in range(2):
-            nc.scalar.copy(h_sbs[0][:, cols(half)], first[half][:])
-        h_banks = [None] + [whole_tile("bank%d" % (4 + t), w_lhs[t], z_words, z_scales) for t in range(1, PACK)]
+            nc.scalar.copy(h_sb[0][:, cols(half)], first[half][:])
+        h_banks = {t: product("bank%d" % (PACK + t), w_lhs[t], z_words, z_scales, slice(0, S)) for t in range(1, PACK)}
 
         out_rows = out.rearrange("(p t) j -> p t j", t=PACK)
-        hop = [keep.tile([P, S], F32, name="hop%d" % t) for t in range(PACK)]
-        st = [keep.tile([P, S], F32, name="st%d" % t) for t in range(PACK)]
-        sent = [keep.tile([P, 2 * S], F32, name="sent%d" % t) for t in range(PACK)]
-        res = [keep.tile([P, S], F32, name="res%d" % t) for t in range(PACK)]
+        hop, st = row_tiles("hop", S), row_tiles("st", S)
+        sent = {t: keep.tile([P, 2 * S], F32, name="sent%d" % t) for t in (0, 1, 3)}
+        res = row_tiles("res", S)
 
-        def fetch(t, lo, hi):
-            nc.scalar.activation(hop[t][:, lo:hi], h_sbs[t][:].indirect(n3_t[:, lo // 16 : hi // 16]), ACT.Copy)
+        def fetch_hop(t, lo, hi):
+            nc.scalar.activation(hop[t][:, lo:hi], h_sb[t][:].indirect(n3_t[:, entries(lo, hi)]), ACT.Copy)
 
         def send(t, lo, hi):
-            nc.vector.tensor_copy(sent[t][:].indirect(n4_t[:, lo // 16 : hi // 16]), st[t][:, lo:hi])
+            nc.vector.tensor_copy(sent[t][:].indirect(n4_t[:, entries(lo, hi)]), st[t][:, lo:hi])
 
-        pieces = ((0, 128), (128, 256), (256, 512))
+        pieces = ((0, S // 4), (S // 4, HALF), (HALF, S))
         for lo, hi in pieces:
-            fetch(0, lo, hi)
+            fetch_hop(0, lo, hi)
         for t in range(1, PACK):
-            nc.scalar.copy(h_sbs[t][:], h_banks[t][:])
-            fetch(t, 0, HALF)
-            fetch(t, HALF, S)
+            nc.scalar.copy(h_sb[t][:], h_banks[t][:])
+            fetch_hop(t, 0, HALF)
+            fetch_hop(t, HALF, S)
+        sent[2] = keep.tile([P, 2 * S], F32, name="sent2", tag="h_sb3")
         for k, (lo, hi) in enumerate(pieces):
-            nc.vector.tensor_tensor(st[0][:, lo:hi], hop[0][:, lo:hi], h_sbs[0][:, lo:hi], ALU.max)
+            nc.vector.tensor_tensor(st[0][:, lo:hi], hop[0][:, lo:hi], h_sb[0][:, lo:hi], ALU.max)
             if k > 0:
                 send(0, *pieces[k - 1])
         send(0, *pieces[-1])
         for t in range(1, PACK):
             nc.vector.tensor_tensor(st[t][:], hop[t][:], h_banks[t][:], ALU.max)
-            nc.gpsimd.tensor_tensor(res[t - 1][:], sent[t - 1][:, 0:S], h_sbs[t - 1][:], ALU.subtract)
-            nc.sync.dma_start(out_rows[:, t - 1, :], res[t - 1][:])
-            send(t, 0, S)
         last = PACK - 1
+        for t in range(PACK):
+            if t > 0:
+                send(t, 0, S)
+            if t < last:
+                nc.gpsimd.tensor_tensor(res[t][:], sent[t][:, 0:S], h_sb[t][:], ALU.subtract)
+                nc.sync.dma_start(out_rows[:, t, :], res[t][:])
         for half, queue in enumerate((nc.sync, nc.scalar)):
             nc.vector.tensor_tensor(res[last][:, cols(half)], sent[last][:, cols(half)], h_banks[last][:, cols(half)], ALU.subtract)
             queue.dma_start(out_rows[:, last, cols(half)], res[last][:, cols(half)])

from contextlib import ExitStack

import concourse.mybir as mybir

F32 = mybir.dt.float32
BF16 = mybir.dt.bfloat16
I32 = mybir.dt.int32
U32 = mybir.dt.uint32
U16 = mybir.dt.uint16
U8 = mybir.dt.uint8
FP8X4 = mybir.dt.float8_e4m3fn_x4
ALU = mybir.AluOpType
ACT = mybir.ActivationFunctionType

P = 128
PACK = 4
TABLE = 2048
S = 512
HALF = 256
LANES = 16
QUAD = 32
RUN = 4
VECTOR_COLS = 336
FLOPS = 2 * 2 * 512 * 512 * 512


def tile_picked_hwlratiosendhop_none_p_kernel(tc, x_words, x_scales, d_words, d_scales, gn, w1, offs, ci, n1, n2, n3, n4, out):
    nc = tc.nc
    with ExitStack() as ctx:
        keep = ctx.enter_context(tc.tile_pool(name="keep", bufs=1))
        shared = ctx.enter_context(tc.tile_pool(name="shared", bufs=1))
        psum = ctx.enter_context(tc.psum_pool(name="psum", bufs=1))

        def load_list(name, src):
            tile = keep.tile(list(src.shape), U16, name=name)
            nc.sync.dma_start(tile[:], src)
            return tile

        def cols(half):
            return slice(half * HALF, (half + 1) * HALF)

        def entries(lo, hi):
            return slice(lo // LANES, hi // LANES)

        def rows(t):
            return slice(t * P, (t + 1) * P)

        def row_tiles(name, width, **placing):
            return [keep.tile([P, width], F32, name="%s%d" % (name, t), **placing) for t in range(PACK)]

        xs_tab = keep.tile([P, TABLE], U8, name="xs_tab")
        ds_tab = shared.tile([P, TABLE], U8, name="ds_tab", offset=0)
        nc.gpsimd.memset(xs_tab[:].bitcast(I32), 0)
        nc.gpsimd.memset(ds_tab[:].bitcast(I32), 0)

        warm_in = keep.tile([P, 1], F32, name="warm_in")
        warm_out = keep.tile([P, 1], F32, name="warm_out")
        nc.vector.memset(warm_in[:], 1.0)
        nc.scalar.activation(warm_out[:], warm_in[:], ACT.Abs_reciprocal_sqrt, bias=0.5)

        offs_t = load_list("offs_t", offs)
        ci_t = load_list("ci_t", ci)
        n2_t = load_list("n2_t", n2)
        n1_t = load_list("n1_t", n1)
        nc.scalar.dma_start(xs_tab[:].bitcast(I32)[0:P:8, :], x_scales[0].bitcast(I32))
        dw_tab = shared.tile([P, TABLE], U32, name="dw_tab", offset=TABLE)
        xw_tab = keep.tile([P, TABLE], U32, name="xw_tab")
        nc.sync.dma_start(dw_tab[:].bitcast(I32), d_words[0].rearrange("p c r -> p (c r)").bitcast(I32))
        n3_t = load_list("n3_t", n3)
        n4_t = load_list("n4_t", n4)
        for j in range(PACK):
            nc.scalar.dma_start(ds_tab[:].bitcast(I32)[j:P:QUAD, :], d_scales[0].bitcast(I32)[j:16:PACK, :])
        nc.gpsimd.dma_start(xw_tab[:].bitcast(I32), x_words[0].rearrange("p c r -> p (c r)").bitcast(I32))

        xs_pick = keep.tile([P, S], U8, name="xs_pick")
        xs_plane = keep.tile([P, S], U8, name="xs_plane", align_bytes=64)
        nc.gpsimd.memset(xs_plane[:].bitcast(I32), 0)
        nc.vector.tensor_copy(xs_pick[:], xs_tab[:].indirect(offs_t[:]))
        for j in range(PACK):
            nc.scalar.dma_start(xs_plane[:].bitcast(I32)[j:P:QUAD, :], xs_pick[:].bitcast(I32)[8 * j : P : QUAD, :])
        gain = keep.tile([P, PACK], F32, name="gain", tag="xs_tab")
        nc.gpsimd.dma_start(gain[:], gn.rearrange("(p t) o -> p (t o)", t=PACK))
        dw_pick = keep.tile([P, S], U32, name="dw_pick", align_bytes=64)
        nc.vector.tensor_copy(dw_pick[:].rearrange("p (t m) -> p m t", t=PACK), dw_tab[:].indirect(ci_t[:]))
        ds_pick = keep.tile([P, S], U8, name="ds_pick", align_bytes=64)
        nc.vector.tensor_copy(ds_pick[:].rearrange("p (t m) -> p m t", t=PACK), ds_tab[:].indirect(ci_t[:]))
        xw_pick = shared.tile([P, S], U32, name="xw_pick", offset=TABLE // 2, align_bytes=64)
        for half in range(2):
            nc.vector.tensor_copy(xw_pick[:, cols(half)], xw_tab[:].indirect(offs_t[:, entries(half * HALF, (half + 1) * HALF)]))

        w_raw = keep.tile([P, PACK, S], F32, name="w_raw", tag="xw_tab")
        nc.sync.dma_start(w_raw[:], w1.rearrange("(p j) n -> p j n", j=PACK))

        def product(bank_name, lhs, rhs_words, rhs_scales, columns):
            bank = psum.tile([P, columns.stop - columns.start], F32, name=bank_name)
            nc.tensor.matmul_mx(out=bank[:], lhsT=lhs[0].bitcast(FP8X4), lhsT_scale=lhs[1],
                                rhs=rhs_words[:, columns].bitcast(FP8X4), rhs_scale=rhs_scales[:, columns], start=True, stop=True)
            return bank

        d_lhs = [(dw_pick[:, rows(t)], ds_pick[:, rows(t)]) for t in range(PACK)]
        s_sb = row_tiles("s_sb", S)
        pa, pb, size, root, recip = [row_tiles(name, HALF) for name in ("pa", "pb", "size", "root", "recip")]
        left = product("bank0", d_lhs[0], xw_pick, xs_plane, cols(0))
        right = product("bank1", d_lhs[0], xw_pick, xs_plane, cols(1))
        nc.scalar.activation(s_sb[0][:, cols(0)], left[:], ACT.Copy, scale=0.0625)
        nc.vector.tensor_scalar_mul(s_sb[0][:, cols(1)], right[:], 0.0625)
        s_banks = {t: product("bank%d" % t, d_lhs[t], xw_pick, xs_plane, slice(0, S)) for t in range(1, PACK)}
        nc.vector.tensor_copy(pa[0][:], s_sb[0][:].indirect(n1_t[:]))
        nc.scalar.activation(pb[0][:], s_sb[0][:].indirect(n2_t[:]), ACT.Copy)

        def leave_bank(t):
            nc.scalar.activation(s_sb[t][:], s_banks[t][:], ACT.Copy, scale=0.0625)

        def fetch_pair(dst, t, list_tile):
            nc.scalar.activation(dst[t][:], s_sb[t][:].indirect(list_tile[:]), ACT.Copy)

        def take_size(t):
            nc.scalar.activation(size[t][:], pb[t][:], ACT.Abs)

        def take_root(t):
            nc.scalar.activation(root[t][:], size[t][:], ACT.Abs_reciprocal_sqrt, bias=0.5)

        def take_square(t):
            nc.scalar.activation(recip[t][:], root[t][:], ACT.Square)

        leave_bank(1)
        take_size(0)
        fetch_pair(pb, 1, n2_t)
        fetch_pair(pa, 1, n1_t)

        leave_bank(2)
        take_root(0)
        fetch_pair(pb, 2, n2_t)
        fetch_pair(pa, 2, n1_t)
        take_square(0)

        leave_bank(3)
        take_size(1)
        fetch_pair(pb, 3, n2_t)
        take_root(1)
        fetch_pair(pa, 3, n1_t)
        take_square(1)

        for step in (take_size, take_root, take_square):
            for t in (2, 3):
                step(t)

        z_planes = keep.tile([P, PACK, S], BF16, name="z_planes")
        larger = row_tiles("larger", HALF)
        placed = row_tiles("placed", S, align_bytes=64)

        def take_larger(t):
            nc.vector.tensor_tensor(larger[t][:], pa[t][:], pb[t][:], ALU.max)

        def put_larger(t):
            nc.vector.tensor_copy(placed[t][:].indirect(n2_t[:]), larger[t][:])

        def put_ratio(t):
            nc.vector.tensor_tensor(placed[t][:].indirect(n1_t[:]), pa[t][:], recip[t][:], ALU.mult)

        def round_plane(t, lo, hi):
            nc.scalar.activation(z_planes[:, t, lo:hi], placed[t][:, lo:hi], ACT.Copy, scale=gain[:, t : t + 1])

        for t in (0, 1):
            take_larger(t)
            put_larger(t)
        for t in (2, 3):
            take_larger(t)
            put_ratio(t - 2)
            put_larger(t)
        put_ratio(2)
        put_ratio(3)

        round_plane(0, 0, S)
        w_il = keep.tile([P, PACK * S], BF16, name="w_il", tag="placed0", align_bytes=64)
        nc.scalar.copy(w_il[:].rearrange("p (t m j) -> p m j t", t=PACK, j=PACK), w_raw[:].rearrange("p j (m t) -> p m j t", t=PACK))
        w0_words = keep.tile([P, P], U32, name="w0_words", align_bytes=64)
        w0_scales = keep.tile([P, P], U8, name="w0_scales", align_bytes=64)
        nc.vector.quantize_mx(out=w0_words[:].bitcast(FP8X4), scales=w0_scales[:], in_=w_il[:, 0 : P * PACK])
        round_plane(1, 0, S)
        round_plane(2, 0, S)
        nc.vector.tensor_scalar_mul(z_planes[:, 3, 0:VECTOR_COLS], placed[3][:, 0:VECTOR_COLS], gain[:, 3:4])
        round_plane(3, VECTOR_COLS, S)

        z_il = keep.tile([P, S * PACK], BF16, name="z_il", align_bytes=64)
        z_words = keep.tile([P, S], U32, name="z_words", align_bytes=64)
        z_scales = keep.tile([P, S], U8, name="z_scales", align_bytes=64)
        z_dst = z_il[:].rearrange("p (c i t) -> p c t i", i=RUN, t=PACK)
        z_src = z_planes[:].rearrange("p t (c i) -> p c t i", i=RUN)
        nc.vector.tensor_copy(z_dst[:, 0 : VECTOR_COLS // RUN], z_src[:, 0 : VECTOR_COLS // RUN])
        nc.scalar.copy(z_dst[:, VECTOR_COLS // RUN : S // RUN], z_src[:, VECTOR_COLS // RUN : S // RUN])
        for half in range(2):
            nc.vector.quantize_mx(out=z_words[:, cols(half)].bitcast(FP8X4), scales=z_scales[:, cols(half)],
                                  in_=z_il[:, half * HALF * PACK : (half + 1) * HALF * PACK])
        wr_words = keep.tile([P, S - P], U32, name="wr_words", tag="z_il", align_bytes=64)
        wr_scales = keep.tile([P, S - P], U8, name="wr_scales", align_bytes=64)
        nc.vector.quantize_mx(out=wr_words[:].bitcast(FP8X4), scales=wr_scales[:], in_=w_il[:, P * PACK : S * PACK])
        w_lhs = [(w0_words[:], w0_scales[:])] + [(wr_words[:, rows(t)], wr_scales[:, rows(t)]) for t in range(PACK - 1)]

        h_sb = row_tiles("h_sb", S)
        first = [product("bank%d" % (PACK + half), w_lhs[0], z_words, z_scales, cols(half)) for half in range(2)]
        for half in range(2):
            nc.scalar.copy(h_sb[0][:, cols(half)], first[half][:])
        h_banks = {t: product("bank%d" % (PACK + t), w_lhs[t], z_words, z_scales, slice(0, S)) for t in range(1, PACK)}

        out_rows = out.rearrange("(p t) j -> p t j", t=PACK)
        hop, st = row_tiles("hop", S), row_tiles("st", S)
        sent = {t: keep.tile([P, 2 * S], F32, name="sent%d" % t) for t in (0, 1, 3)}
        res = row_tiles("res", S)

        def fetch_hop(t, lo, hi):
            nc.scalar.activation(hop[t][:, lo:hi], h_sb[t][:].indirect(n3_t[:, entries(lo, hi)]), ACT.Copy)

        def send(t, lo, hi):
            nc.vector.tensor_copy(sent[t][:].indirect(n4_t[:, entries(lo, hi)]), st[t][:, lo:hi])

        pieces = ((0, S // 4), (S // 4, HALF), (HALF, S))
        for lo, hi in pieces:
            fetch_hop(0, lo, hi)
        for t in range(1, PACK):
            nc.scalar.copy(h_sb[t][:], h_banks[t][:])
            fetch_hop(t, 0, HALF)
            fetch_hop(t, HALF, S)
        sent[2] = keep.tile([P, 2 * S], F32, name="sent2", tag="h_sb3")
        for k, (lo, hi) in enumerate(pieces):
            nc.vector.tensor_tensor(st[0][:, lo:hi], hop[0][:, lo:hi], h_sb[0][:, lo:hi], ALU.max)
            if k > 0:
                send(0, *pieces[k - 1])
        send(0, *pieces[-1])
        for t in range(1, PACK):
            nc.vector.tensor_tensor(st[t][:], hop[t][:], h_banks[t][:], ALU.max)
        last = PACK - 1
        for t in range(PACK):
            if t > 0:
                send(t, 0, S)
            if t < last:
                nc.gpsimd.tensor_tensor(res[t][:], sent[t][:, 0:S], h_sb[t][:], ALU.subtract)
                nc.sync.dma_start(out_rows[:, t, :], res[t][:])
        for half, queue in enumerate((nc.sync, nc.scalar)):
            nc.vector.tensor_tensor(res[last][:, cols(half)], sent[last][:, cols(half)], h_banks[last][:, cols(half)], ALU.subtract)
            queue.dma_start(out_rows[:, last, cols(half)], res[last][:, cols(half)])
